import numpy as np
import ml_dtypes


def mxq(x, axis, fmt="e4m3"):
    dtype, down = {"e4m3": (ml_dtypes.float8_e4m3fn, 7), "e5m2": (ml_dtypes.float8_e5m2, 14)}[fmt]
    v = np.moveaxis(np.asarray(x, np.float32).astype(ml_dtypes.bfloat16).astype(np.float64), axis, -1)
    blocks = v.reshape(v.shape[:-1] + (-1, 32))
    amax = np.abs(blocks).max(-1, keepdims=True)
    byte = np.maximum(np.where(amax > 0, np.frexp(amax)[1] - 1 + 127, 0) - down, 1)
    scale = np.exp2(byte - 127.0)
    codes = (blocks / scale).astype(np.float32).astype(dtype).astype(np.float64)
    return np.moveaxis((codes * scale).reshape(v.shape), -1, axis)


WIDE = False


def mx_kscale(k):
    if not WIDE:
        return np.ones(k)
    levels = np.array([10, -10, 5, -5, 0])
    if k % 512:
        return np.exp2(np.random.permutation(np.resize(levels, k // 32))).repeat(32)
    a = np.empty((k // 512, 16))
    for p in range(k // 512):
        a[p, :8] = np.random.permutation(np.resize(levels, 8))
        for g in range(8):
            far = levels[np.abs(levels - a[p, g]) >= 10]
            a[p, g + 8] = far[np.random.randint(len(far))]
    return np.exp2(a.ravel()).repeat(32)


def f64(x):
    return np.asarray(x).astype(np.float64)


def striped(idx):
    return np.tile(idx.reshape(-1, 16).T, (8, 1)).astype(np.uint16)


def unstriped(offs):
    return offs[:16].T.reshape(-1).astype(np.int64)


def striped8(idx):
    return np.concatenate([x.reshape(-1, 16).T for x in idx]).astype(np.uint16)


def runs(offs, k):
    lists = np.stack([offs[16 * r : 16 * r + 16].T.reshape(-1) for r in range(8)]).astype(np.int64)
    return lists[np.arange(k) % 512 // 64]


def pack_weight(w):
    k, n = w.shape
    w = f64(np.asarray(w, np.float32).astype(ml_dtypes.bfloat16)).reshape(k // 32, 32, n)
    amax = np.abs(w).max(1)
    byte = np.clip(np.where(amax > 0, np.frexp(amax)[1] - 1 + 127 - 7, 1), 1, 254)
    scaled = (w * np.exp2(127.0 - byte)[:, None, :]).reshape(k, n).astype(np.float32)
    words = np.ascontiguousarray(scaled.reshape(k // 512, 128, 4, n).transpose(0, 1, 3, 2)).astype(ml_dtypes.float8_e4m3fn).view(np.uint8)
    return words, np.ascontiguousarray(byte.astype(np.uint8).reshape(k // 512, 16, n))


def unpack_weight(words, scales):
    g, p, n, _ = words.shape
    vals = np.ascontiguousarray(words).view(ml_dtypes.float8_e4m3fn).astype(np.float64) * np.repeat(np.exp2(scales.astype(np.float64) - 127.0), 8, axis=1)[..., None]
    return vals.transpose(0, 1, 3, 2).reshape(g * 512, n)


K, T, S, N, H = 512, 2048, 512, 512, 512


def setup_inputs():
    n = np.random.standard_normal
    s = mx_kscale(K)[:, None]
    u = mx_kscale(H)
    packed_xT = pack_weight(n((K, T)) * s)
    return {
        "x_words": packed_xT[0],
        "x_scales": packed_xT[1],
        "w1": (n((K, H)) / np.sqrt(K) / s).astype(np.float32),
        "gn": (np.random.uniform(0.5, 1.5, (H, 1)) * u[:, None]).astype(np.float32),
        "w2": (n((H, N)) / np.sqrt(2 * H) / u[:, None]).astype(np.float32),
        "w3": (n((K, N)) / np.sqrt(2 * K) / s).astype(np.float32),
        "offs": striped(np.random.permutation(T)[:S]),
        "n1": striped8(np.stack([np.random.permutation(S) for _ in range(8)])),
        "n2": striped8(np.stack([np.random.permutation(S) for _ in range(8)])),
        "n3": striped8(np.stack([np.random.permutation(S) for _ in range(8)])),
        "hz": striped8(np.random.randint(0, T, (8, S))),
        "n4": striped8(np.stack([np.random.permutation(S) for _ in range(8)])),
        "n5": striped8(np.stack([np.random.permutation(S) for _ in range(8)])),
        "n6": striped8(np.stack([np.random.permutation(S) for _ in range(8)])),
    }


def reference(x_words, x_scales, w1, gn, w2, w3, offs, n1, n2, n3, hz, n4, n5, n6):
    xq = unpack_weight(x_words, x_scales)[:, unstriped(offs)]
    y = mxq(f64(w1), 0, "e4m3").T @ xq
    z = f64(gn) * (y + y[np.arange(H)[:, None], runs(n1, H)] - (np.maximum(y[np.arange(H)[:, None], runs(n2, H)], y[np.arange(H)[:, None], runs(n3, H)])))
    x_hz = unpack_weight(x_words, x_scales)[np.arange(K)[:, None], runs(hz, K)]
    h = mxq(f64(w2), 0, "e4m3").T @ mxq(z, 0, "e4m3") + mxq(f64(w3), 0, "e4m3").T @ x_hz
    return 0.75 * (h * (h[np.arange(N)[:, None], runs(n4, N)]) + (h[np.arange(N)[:, None], runs(n5, N)]) * (h[np.arange(N)[:, None], runs(n6, N)]))

@@ -1,0 +1,242 @@
+from contextlib import ExitStack
+
+import concourse.mybir as mybir
+
+K, T, S, H, N = 512, 2048, 512, 512, 512
+FLOPS = 2 * S * (K * H + H * N + K * N)
+
+F32 = mybir.dt.float32
+BF16 = mybir.dt.bfloat16
+I32 = mybir.dt.int32
+U32 = mybir.dt.uint32
+U16 = mybir.dt.uint16
+U8 = mybir.dt.uint8
+FP8X4 = mybir.dt.float8_e4m3fn_x4
+ALU = mybir.AluOpType
+COPY = mybir.ActivationFunctionType.Copy
+
+P = 128
+PACK = 4
+HALF = S // 2
+W1_SCALAR_COLUMNS = 96
+
+
+def tile_picked_mixhtrimdot_none_p_kernel(
+    tc, x_words, x_scales, w1, gn, w2, w3, offs, n1, n2, n3, hz, n4, n5, n6, out
+):
+    nc = tc.nc
+    with ExitStack() as ctx:
+        lists = ctx.enter_context(tc.tile_pool(name="lists", bufs=1))
+        keep = ctx.enter_context(tc.tile_pool(name="keep", bufs=1))
+        ring = ctx.enter_context(tc.tile_pool(name="ring", bufs=3))
+        psum = ctx.enter_context(tc.psum_pool(name="psum", bufs=1))
+
+        def load_list(name, dram):
+            tile = lists.tile([P, S // 16], U16, name=name)
+            nc.sync.dma_start(tile[:], dram)
+            return tile
+
+        def load_weight(name, dram):
+            raw = keep.tile([P, PACK, dram.shape[1]], F32, name=name, align_bytes=64)
+            nc.sync.dma_start(raw[:], dram.rearrange("(p j) c -> p j c", j=PACK))
+            return raw
+
+        def entries(tile, cols):
+            return tile[:, cols.start // 16 : cols.stop // 16]
+
+        scale_table = keep.tile([P, T], U8, name="scale_table", align_bytes=64)
+        nc.gpsimd.memset(scale_table[:].bitcast(I32), 0)
+        hz_scales = keep.tile([P, S], U8, name="hz_scales", align_bytes=64)
+        nc.gpsimd.memset(hz_scales[:].bitcast(I32), 0)
+
+        offs_t = load_list("offs_t", offs)
+        w1_raw = load_weight("w1_raw", w1)
+        scale_rows = x_scales[0].bitcast(I32)
+        table_words = scale_table[:].bitcast(I32)
+        for r in range(2):
+            nc.sync.dma_start(table_words[r:P:32, :], scale_rows[r:16:4, :])
+        for r in range(2, 4):
+            nc.sync.dma_start(
+                table_words[r:P:16, :], scale_rows[r:16:4, :].unsqueeze(1).broadcast_to([4, 2, T // 4])
+            )
+        word_table = keep.tile([P, T], I32, name="word_table", align_bytes=64)
+        nc.sync.dma_start(word_table[:], x_words[0].rearrange("p n t -> p (n t)").bitcast(I32))
+        gain = keep.tile([P, PACK], F32, name="gain")
+        nc.sync.dma_start(gain[:], gn.rearrange("(p t) o -> p (t o)", t=PACK))
+        n2_t = load_list("n2_t", n2)
+        n3_t = load_list("n3_t", n3)
+        n1_t = load_list("n1_t", n1)
+        hz_t = load_list("hz_t", hz)
+        w3_raw = load_weight("w3_raw", w3)
+        w2_raw = load_weight("w2_raw", w2)
+        n4_t = load_list("n4_t", n4)
+        n5_t = load_list("n5_t", n5)
+        n6_t = load_list("n6_t", n6)
+
+        def weight_tiles(name):
+            return (
+                keep.tile([P, PACK, P, PACK], BF16, name=name + "_bf", align_bytes=64),
+                keep.tile([P, PACK * P], U32, name=name + "_codes", align_bytes=64),
+                keep.tile([P, PACK * P], U8, name=name + "_scales", align_bytes=64),
+            )
+
+        def deal(copy, rounded, raw, m):
+            copy(
+                rounded[:, :, m, :].rearrange("p t m j -> p m j t"),
+                raw[:].rearrange("p j (m t) -> p m j t", t=PACK)[:, m, :, :],
+            )
+
+        def quantize_weight(rounded, codes, scales):
+            nc.vector.quantize_mx(
+                out=codes[:].bitcast(FP8X4), scales=scales[:], in_=rounded[:].rearrange("p t m j -> p (t m j)")
+            )
+
+        w1_bf, w1_codes, w1_scales = weight_tiles("w1")
+        deal(nc.scalar.copy, w1_bf, w1_raw, slice(0, W1_SCALAR_COLUMNS))
+        deal(nc.vector.tensor_copy, w1_bf, w1_raw, slice(W1_SCALAR_COLUMNS, P))
+        xq_scales = keep.tile([P, S], U8, name="xq_scales", align_bytes=64)
+        nc.vector.tensor_copy(xq_scales[:], scale_table[:].indirect(offs_t[:]))
+        quantize_weight(w1_bf, w1_codes, w1_scales)
+        xq_words = keep.tile([P, S], U32, name="xq_words", align_bytes=64)
+        halves = [slice(0, HALF), slice(HALF, S)]
+        for cols in halves:
+            nc.vector.tensor_copy(xq_words[:, cols], word_table[:].bitcast(U32).indirect(entries(offs_t, cols)))
+
+        def product(acc, codes, scales, t, words, word_scales, start, stop):
+            m = slice(t * P, (t + 1) * P)
+            nc.tensor.matmul_mx(
+                out=acc,
+                lhsT=codes[:, m].bitcast(FP8X4),
+                lhsT_scale=scales[:, m],
+                rhs=words.bitcast(FP8X4),
+                rhs_scale=word_scales,
+                start=start,
+                stop=stop,
+            )
+
+        whole = slice(0, S)
+        y_parts = [(0, cols) for cols in halves] + [(t, whole) for t in range(1, PACK)]
+        y_bank = {}
+        for t, cols in y_parts:
+            tag = "early0" if cols.stop < S else "late%d" % t
+            y_bank[t, cols.start] = psum.tile([P, cols.stop - cols.start], F32, name="y_bank", tag=tag)
+            product(y_bank[t, cols.start][:], w1_codes, w1_scales, t, xq_words[:, cols], xq_scales[:, cols], True, True)
+
+        hz_picked = keep.tile([P, S], U8, name="hz_picked", align_bytes=64)
+        nc.vector.tensor_copy(hz_picked[:], scale_table[:].indirect(hz_t[:]))
+        for r in range(4):
+            first = r if r < 2 else 16 + r
+            nc.sync.dma_start(hz_scales[:].bitcast(I32)[r:P:32, :], hz_picked[:].bitcast(I32)[first:P:32, :])
+        hz_words = keep.tile([P, S], U32, name="hz_words", align_bytes=64)
+        nc.vector.tensor_copy(hz_words[:], word_table[:].bitcast(U32).indirect(hz_t[:]))
+        w2_bf, w2_codes, w2_scales = weight_tiles("w2")
+        w3_bf, w3_codes, w3_scales = weight_tiles("w3")
+        deal(nc.vector.tensor_copy, w3_bf, w3_raw, slice(0, P))
+        quantize_weight(w3_bf, w3_codes, w3_scales)
+        deal(nc.vector.tensor_copy, w2_bf, w2_raw, slice(0, P))
+
+        window = [keep.tile([P, 2 * S], F32, name="window%d" % t) for t in range(PACK)]
+        z_rows = keep.tile([P, 2, PACK, HALF], BF16, name="z_rows", align_bytes=64)
+        units = [(0, whole), (1, whole)] + [(t, cols) for cols in halves for t in (2, 3)]
+
+        def by_half(ap):
+            return ap.rearrange("p (s c) -> p s c", c=HALF)
+
+        def look_up(name, t, offsets, cols):
+            picked = ring.tile([P, cols.stop - cols.start], F32, name=name)
+            nc.scalar.activation(picked[:], window[t][:].indirect(entries(offsets, cols)), COPY)
+            return picked
+
+        def combine(u, t, cols, y2, y3, between):
+            width = cols.stop - cols.start
+            larger = keep.tile([P, width], F32, name="larger", tag=("w2_raw", "w2_bf")[u % 2], align_bytes=64)
+            nc.vector.tensor_tensor(larger[:], y2[:], y3[:], ALU.max)
+            between[0]()
+            rest = ring.tile([P, width], F32, name="rest")
+            nc.vector.tensor_tensor(rest[:], window[t][:].indirect(entries(n1_t, cols)), larger[:], ALU.subtract)
+            between[1]()
+
+            def scale():
+                nc.vector.scalar_tensor_tensor(
+                    z_rows[:, cols.start // HALF : cols.stop // HALF, t, :],
+                    by_half(rest[:]),
+                    gain[:, t : t + 1],
+                    by_half(window[t][:, S + cols.start : S + cols.stop]),
+                    ALU.mult,
+                    ALU.add,
+                )
+
+            return scale
+
+        z_codes = [keep.tile([P, HALF], U32, name="z_codes%d" % s, align_bytes=64) for s in range(2)]
+        z_scales = [keep.tile([P, HALF], U8, name="z_scales%d" % s, align_bytes=64) for s in range(2)]
+        z_bf = [keep.tile([P, HALF, PACK], BF16, name="z_bf%d" % s, align_bytes=64) for s in range(2)]
+
+        def interleave(copy, s, a=0, b=HALF // 8):
+            copy(
+                z_bf[s][:].rearrange("p (c i) t -> p c t i", i=8)[:, a:b],
+                z_rows[:, s, :, :].rearrange("p t (c i) -> p c t i", i=8)[:, a:b],
+            )
+
+        def second_product(s, copies):
+            cols = halves[s]
+            nc.vector.quantize_mx(
+                out=z_codes[s][:].bitcast(FP8X4), scales=z_scales[s][:], in_=z_bf[s][:].rearrange("p c t -> p (c t)")
+            )
+            banks = []
+            for t in range(PACK):
+                bank = psum.tile([P, HALF], F32, name="h_bank%d_%d" % (s, t), tag=("early%d", "late%d")[s] % t)
+                product(bank[:], w3_codes, w3_scales, t, hz_words[:, cols], hz_scales[:, cols], True, False)
+                product(bank[:], w2_codes, w2_scales, t, z_codes[s][:], z_scales[s][:], False, True)
+                banks.append(bank)
+                if t < len(copies):
+                    copies[t](window[t][:, cols], bank[:])
+            return banks
+
+        def nothing():
+            return None
+
+        pending = lambda: quantize_weight(w2_bf, w2_codes, w2_scales)
+        for u, (t, cols) in enumerate(units):
+            if cols.start == 0:
+                for part in [c for p, c in y_parts if p == t]:
+                    bank = y_bank[t, part.start]
+                    nc.scalar.copy(window[t][:, part], bank[:])
+                    if t == 1:
+                        nc.vector.tensor_scalar(window[t][:, S:], window[t][:, :S], gain[:, t : t + 1], None, ALU.mult)
+                    else:
+                        nc.scalar.activation(
+                            window[t][:, S + part.start : S + part.stop], bank[:], COPY, scale=gain[:, t : t + 1]
+                        )
+            y2 = look_up("y2", t, n2_t, cols)
+            y3 = look_up("y3", t, n3_t, cols)
+            pending = combine(u, t, cols, y2, y3, (pending, nothing))
+        interleave(nc.scalar.copy, 0)
+        second_product(0, [nc.scalar.copy] * PACK)
+        pending()
+        interleave(nc.vector.tensor_copy, 1, 0, 22)
+        interleave(nc.scalar.copy, 1, 22, 32)
+        late_banks = second_product(1, [nc.vector.tensor_copy] * 4)
+
+        out_rows = out.rearrange("(p t) j -> p t j", t=PACK)
+        pending = nothing
+        units = [(t, cols) for t in range(PACK) for cols in halves]
+        for t, cols in units:
+            width = cols.stop - cols.start
+            if t >= 4-0 and t+0<PACK and cols.start == 0:
+                nc.scalar.copy(window[t+0][:, halves[1]], late_banks[t+0][:])
+            h5 = look_up("h5", t, n5_t, cols)
+            h4 = look_up("h4", t, n4_t, cols)
+            far = ring.tile([P, width], F32, name="far")
+            nc.vector.tensor_tensor(far[:], window[t][:].indirect(entries(n6_t, cols)), h5[:], ALU.mult)
+            pending()
+            near = ring.tile([P, width], F32, name="near")
+            nc.vector.scalar_tensor_tensor(near[:], h4[:], 0.75, window[t][:, cols], ALU.mult, ALU.mult)
+
+            def store(t=t, cols=cols, width=width, far=far, near=near):
+                result = ring.tile([P, width], F32, name="result")
+                nc.vector.scalar_tensor_tensor(result[:], far[:], 0.75, near[:], ALU.mult, ALU.add)
+                nc.sync.dma_start(out_rows[:, t, cols], result[:])
+
+            pending = store
+        pending()

@@ -18,7 +18,7 @@ COPY = mybir.ActivationFunctionType.Copy
 P = 128
 PACK = 4
 HALF = S // 2
-W1_SCALAR_COLUMNS = 96
+W1_SCALAR_COLUMNS = 56
 
 
 def tile_picked_mixhtrimdot_none_p_kernel(
@@ -50,7 +50,7 @@ def tile_picked_mixhtrimdot_none_p_kernel(
         nc.gpsimd.memset(hz_scales[:].bitcast(I32), 0)
 
         offs_t = load_list("offs_t", offs)
-        w1_raw = load_weight("w1_raw", w1)
+        hz_t = load_list("hz_t", hz)
         scale_rows = x_scales[0].bitcast(I32)
         table_words = scale_table[:].bitcast(I32)
         for r in range(2):
@@ -59,6 +59,7 @@ def tile_picked_mixhtrimdot_none_p_kernel(
             nc.sync.dma_start(
                 table_words[r:P:16, :], scale_rows[r:16:4, :].unsqueeze(1).broadcast_to([4, 2, T // 4])
             )
+        w1_raw = load_weight("w1_raw", w1)
         word_table = keep.tile([P, T], I32, name="word_table", align_bytes=64)
         nc.sync.dma_start(word_table[:], x_words[0].rearrange("p n t -> p (n t)").bitcast(I32))
         gain = keep.tile([P, PACK], F32, name="gain")
@@ -66,7 +67,6 @@ def tile_picked_mixhtrimdot_none_p_kernel(
         n2_t = load_list("n2_t", n2)
         n3_t = load_list("n3_t", n3)
         n1_t = load_list("n1_t", n1)
-        hz_t = load_list("hz_t", hz)
         w3_raw = load_weight("w3_raw", w3)
         w2_raw = load_weight("w2_raw", w2)
         n4_t = load_list("n4_t", n4)
@@ -91,11 +91,16 @@ def tile_picked_mixhtrimdot_none_p_kernel(
                 out=codes[:].bitcast(FP8X4), scales=scales[:], in_=rounded[:].rearrange("p t m j -> p (t m j)")
             )
 
+        xq_scales = keep.tile([P, S], U8, name="xq_scales", align_bytes=64)
+        nc.vector.tensor_copy(xq_scales[:], scale_table[:].indirect(offs_t[:]))
+        hz_picked = keep.tile([P, S], U8, name="hz_picked", align_bytes=64)
+        nc.vector.tensor_copy(hz_picked[:], scale_table[:].indirect(hz_t[:]))
+        for r in range(4):
+            first = r if r < 2 else 16 + r
+            nc.sync.dma_start(hz_scales[:].bitcast(I32)[r:P:32, :], hz_picked[:].bitcast(I32)[first:P:32, :])
         w1_bf, w1_codes, w1_scales = weight_tiles("w1")
         deal(nc.scalar.copy, w1_bf, w1_raw, slice(0, W1_SCALAR_COLUMNS))
         deal(nc.vector.tensor_copy, w1_bf, w1_raw, slice(W1_SCALAR_COLUMNS, P))
-        xq_scales = keep.tile([P, S], U8, name="xq_scales", align_bytes=64)
-        nc.vector.tensor_copy(xq_scales[:], scale_table[:].indirect(offs_t[:]))
         quantize_weight(w1_bf, w1_codes, w1_scales)
         xq_words = keep.tile([P, S], U32, name="xq_words", align_bytes=64)
         halves = [slice(0, HALF), slice(HALF, S)]
@@ -122,11 +127,6 @@ def tile_picked_mixhtrimdot_none_p_kernel(
             y_bank[t, cols.start] = psum.tile([P, cols.stop - cols.start], F32, name="y_bank", tag=tag)
             product(y_bank[t, cols.start][:], w1_codes, w1_scales, t, xq_words[:, cols], xq_scales[:, cols], True, True)
 
-        hz_picked = keep.tile([P, S], U8, name="hz_picked", align_bytes=64)
-        nc.vector.tensor_copy(hz_picked[:], scale_table[:].indirect(hz_t[:]))
-        for r in range(4):
-            first = r if r < 2 else 16 + r
-            nc.sync.dma_start(hz_scales[:].bitcast(I32)[r:P:32, :], hz_picked[:].bitcast(I32)[first:P:32, :])
         hz_words = keep.tile([P, S], U32, name="hz_words", align_bytes=64)
         nc.vector.tensor_copy(hz_words[:], word_table[:].bitcast(U32).indirect(hz_t[:]))
         w2_bf, w2_codes, w2_scales = weight_tiles("w2")
@@ -172,10 +172,10 @@ def tile_picked_mixhtrimdot_none_p_kernel(
         z_scales = [keep.tile([P, HALF], U8, name="z_scales%d" % s, align_bytes=64) for s in range(2)]
         z_bf = [keep.tile([P, HALF, PACK], BF16, name="z_bf%d" % s, align_bytes=64) for s in range(2)]
 
-        def interleave(copy, s, a=0, b=HALF // 8):
+        def interleave(copy, s):
             copy(
-                z_bf[s][:].rearrange("p (c i) t -> p c t i", i=8)[:, a:b],
-                z_rows[:, s, :, :].rearrange("p t (c i) -> p c t i", i=8)[:, a:b],
+                z_bf[s][:].rearrange("p (c i) t -> p c t i", i=8),
+                z_rows[:, s, :, :].rearrange("p t (c i) -> p c t i", i=8),
             )
 
         def second_product(s, copies):
@@ -193,29 +193,37 @@ def tile_picked_mixhtrimdot_none_p_kernel(
                     copies[t](window[t][:, cols], bank[:])
             return banks
 
+        def leave_bank(t):
+            for part in [c for p, c in y_parts if p == t]:
+                bank = y_bank[t, part.start]
+                if t in (1,):
+                    nc.vector.tensor_copy(window[t][:, part], bank[:])
+                else:
+                    nc.scalar.copy(window[t][:, part], bank[:])
+                if t in (1,):
+                    nc.vector.tensor_scalar(window[t][:, S:], window[t][:, :S], gain[:, t : t + 1], None, ALU.mult)
+                else:
+                    nc.scalar.activation(
+                        window[t][:, S + part.start : S + part.stop], bank[:], COPY, scale=gain[:, t : t + 1]
+                    )
+
         def nothing():
             return None
 
         pending = lambda: quantize_weight(w2_bf, w2_codes, w2_scales)
         for u, (t, cols) in enumerate(units):
-            if cols.start == 0:
-                for part in [c for p, c in y_parts if p == t]:
-                    bank = y_bank[t, part.start]
-                    nc.scalar.copy(window[t][:, part], bank[:])
-                    if t == 1:
-                        nc.vector.tensor_scalar(window[t][:, S:], window[t][:, :S], gain[:, t : t + 1], None, ALU.mult)
-                    else:
-                        nc.scalar.activation(
-                            window[t][:, S + part.start : S + part.stop], bank[:], COPY, scale=gain[:, t : t + 1]
-                        )
+            if cols.start == 0 and t not in (1,):
+                leave_bank(t)
+            if t == 0:
+                for later in (1,):
+                    leave_bank(later)
             y2 = look_up("y2", t, n2_t, cols)
             y3 = look_up("y3", t, n3_t, cols)
             pending = combine(u, t, cols, y2, y3, (pending, nothing))
         interleave(nc.scalar.copy, 0)
         second_product(0, [nc.scalar.copy] * PACK)
         pending()
-        interleave(nc.vector.tensor_copy, 1, 0, 22)
-        interleave(nc.scalar.copy, 1, 22, 32)
+        interleave(nc.vector.tensor_copy, 1)
         late_banks = second_product(1, [nc.vector.tensor_copy] * 4)
 
         out_rows = out.rearrange("(p t) j -> p t j", t=PACK)
@@ -223,8 +231,8 @@ def tile_picked_mixhtrimdot_none_p_kernel(
         units = [(t, cols) for t in range(PACK) for cols in halves]
         for t, cols in units:
             width = cols.stop - cols.start
-            if t >= 4-0 and t+0<PACK and cols.start == 0:
-                nc.scalar.copy(window[t+0][:, halves[1]], late_banks[t+0][:])
+            if t + 0 >= 4 and t + 0 < PACK and cols.start == 0:
+                nc.scalar.copy(window[t + 0][:, halves[1]], late_banks[t + 0][:])
             h5 = look_up("h5", t, n5_t, cols)
             h4 = look_up("h4", t, n4_t, cols)
             far = ring.tile([P, width], F32, name="far")
@@ -234,7 +242,7 @@ def tile_picked_mixhtrimdot_none_p_kernel(
             nc.vector.scalar_tensor_tensor(near[:], h4[:], 0.75, window[t][:, cols], ALU.mult, ALU.mult)
 
             def store(t=t, cols=cols, width=width, far=far, near=near):
-                result = ring.tile([P, width], F32, name="result")
+                result = keep.tile([P, width], F32, name="result%d_%d" % (t, cols.start))
                 nc.vector.scalar_tensor_tensor(result[:], far[:], 0.75, near[:], ALU.mult, ALU.add)
                 nc.sync.dma_start(out_rows[:, t, cols], result[:])
 

@@ -17,8 +17,14 @@ COPY = mybir.ActivationFunctionType.Copy
 
 P = 128
 PACK = 4
+QUADRANT = 32
+GROUP = 16
 HALF = S // 2
-W1_SCALAR_COLUMNS = 56
+WHOLE = slice(0, S)
+HALVES = (slice(0, HALF), slice(HALF, S))
+LINE_BF16 = 8
+RING = 3
+W1_ON_SCALAR = 96
 
 
 def tile_picked_mixhtrimdot_none_p_kernel(
@@ -28,11 +34,11 @@ def tile_picked_mixhtrimdot_none_p_kernel(
     with ExitStack() as ctx:
         lists = ctx.enter_context(tc.tile_pool(name="lists", bufs=1))
         keep = ctx.enter_context(tc.tile_pool(name="keep", bufs=1))
-        ring = ctx.enter_context(tc.tile_pool(name="ring", bufs=3))
+        ring = ctx.enter_context(tc.tile_pool(name="ring", bufs=RING))
         psum = ctx.enter_context(tc.psum_pool(name="psum", bufs=1))
 
         def load_list(name, dram):
-            tile = lists.tile([P, S // 16], U16, name=name)
+            tile = lists.tile([P, S // GROUP], U16, name=name)
             nc.sync.dma_start(tile[:], dram)
             return tile
 
@@ -41,8 +47,8 @@ def tile_picked_mixhtrimdot_none_p_kernel(
             nc.sync.dma_start(raw[:], dram.rearrange("(p j) c -> p j c", j=PACK))
             return raw
 
-        def entries(tile, cols):
-            return tile[:, cols.start // 16 : cols.stop // 16]
+        def entries(list_tile, cols):
+            return list_tile[:, cols.start // GROUP : cols.stop // GROUP]
 
         scale_table = keep.tile([P, T], U8, name="scale_table", align_bytes=64)
         nc.gpsimd.memset(scale_table[:].bitcast(I32), 0)
@@ -50,18 +56,17 @@ def tile_picked_mixhtrimdot_none_p_kernel(
         nc.gpsimd.memset(hz_scales[:].bitcast(I32), 0)
 
         offs_t = load_list("offs_t", offs)
-        hz_t = load_list("hz_t", hz)
-        scale_rows = x_scales[0].bitcast(I32)
-        table_words = scale_table[:].bitcast(I32)
-        for r in range(2):
-            nc.sync.dma_start(table_words[r:P:32, :], scale_rows[r:16:4, :])
-        for r in range(2, 4):
-            nc.sync.dma_start(
-                table_words[r:P:16, :], scale_rows[r:16:4, :].unsqueeze(1).broadcast_to([4, 2, T // 4])
-            )
         w1_raw = load_weight("w1_raw", w1)
+        scale_rows = x_scales[0].bitcast(I32)
+        table_rows = scale_table[:].bitcast(I32)
+        for r in range(PACK // 2):
+            nc.sync.dma_start(table_rows[r:P:QUADRANT, :], scale_rows[r:16:PACK, :])
+        for r in range(PACK // 2, PACK):
+            twice = scale_rows[r:16:PACK, :].unsqueeze(1).broadcast_to([P // QUADRANT, 2, T // 4])
+            nc.sync.dma_start(table_rows[r:P:GROUP, :], twice)
         word_table = keep.tile([P, T], I32, name="word_table", align_bytes=64)
         nc.sync.dma_start(word_table[:], x_words[0].rearrange("p n t -> p (n t)").bitcast(I32))
+        hz_t = load_list("hz_t", hz)
         gain = keep.tile([P, PACK], F32, name="gain")
         nc.sync.dma_start(gain[:], gn.rearrange("(p t) o -> p (t o)", t=PACK))
         n2_t = load_list("n2_t", n2)
@@ -80,37 +85,22 @@ def tile_picked_mixhtrimdot_none_p_kernel(
                 keep.tile([P, PACK * P], U8, name=name + "_scales", align_bytes=64),
             )
 
-        def deal(copy, rounded, raw, m):
+        def round_and_deal(copy, rounded, raw, m):
             copy(
                 rounded[:, :, m, :].rearrange("p t m j -> p m j t"),
                 raw[:].rearrange("p j (m t) -> p m j t", t=PACK)[:, m, :, :],
             )
 
+        def quantize(rounded, codes, scales):
+            nc.vector.quantize_mx(out=codes[:].bitcast(FP8X4), scales=scales[:], in_=rounded)
+
         def quantize_weight(rounded, codes, scales):
-            nc.vector.quantize_mx(
-                out=codes[:].bitcast(FP8X4), scales=scales[:], in_=rounded[:].rearrange("p t m j -> p (t m j)")
-            )
+            quantize(rounded[:].rearrange("p t m j -> p (t m j)"), codes, scales)
 
-        xq_scales = keep.tile([P, S], U8, name="xq_scales", align_bytes=64)
-        nc.vector.tensor_copy(xq_scales[:], scale_table[:].indirect(offs_t[:]))
-        hz_picked = keep.tile([P, S], U8, name="hz_picked", align_bytes=64)
-        nc.vector.tensor_copy(hz_picked[:], scale_table[:].indirect(hz_t[:]))
-        for r in range(4):
-            first = r if r < 2 else 16 + r
-            nc.sync.dma_start(hz_scales[:].bitcast(I32)[r:P:32, :], hz_picked[:].bitcast(I32)[first:P:32, :])
-        w1_bf, w1_codes, w1_scales = weight_tiles("w1")
-        deal(nc.scalar.copy, w1_bf, w1_raw, slice(0, W1_SCALAR_COLUMNS))
-        deal(nc.vector.tensor_copy, w1_bf, w1_raw, slice(W1_SCALAR_COLUMNS, P))
-        quantize_weight(w1_bf, w1_codes, w1_scales)
-        xq_words = keep.tile([P, S], U32, name="xq_words", align_bytes=64)
-        halves = [slice(0, HALF), slice(HALF, S)]
-        for cols in halves:
-            nc.vector.tensor_copy(xq_words[:, cols], word_table[:].bitcast(U32).indirect(entries(offs_t, cols)))
-
-        def product(acc, codes, scales, t, words, word_scales, start, stop):
+        def product(bank, codes, scales, t, words, word_scales, start, stop):
             m = slice(t * P, (t + 1) * P)
             nc.tensor.matmul_mx(
-                out=acc,
+                out=bank[:],
                 lhsT=codes[:, m].bitcast(FP8X4),
                 lhsT_scale=scales[:, m],
                 rhs=words.bitcast(FP8X4),
@@ -119,132 +109,132 @@ def tile_picked_mixhtrimdot_none_p_kernel(
                 stop=stop,
             )
 
-        whole = slice(0, S)
-        y_parts = [(0, cols) for cols in halves] + [(t, whole) for t in range(1, PACK)]
-        y_bank = {}
-        for t, cols in y_parts:
-            tag = "early0" if cols.stop < S else "late%d" % t
-            y_bank[t, cols.start] = psum.tile([P, cols.stop - cols.start], F32, name="y_bank", tag=tag)
-            product(y_bank[t, cols.start][:], w1_codes, w1_scales, t, xq_words[:, cols], xq_scales[:, cols], True, True)
+        def psum_bank(name, t, cols):
+            tag = ("first%d" if cols.stop < S else "second%d") % t
+            return psum.tile([P, cols.stop - cols.start], F32, name=name, tag=tag)
 
-        hz_words = keep.tile([P, S], U32, name="hz_words", align_bytes=64)
-        nc.vector.tensor_copy(hz_words[:], word_table[:].bitcast(U32).indirect(hz_t[:]))
+        w1_bf, w1_codes, w1_scales = weight_tiles("w1")
+        round_and_deal(nc.scalar.copy, w1_bf, w1_raw, slice(0, W1_ON_SCALAR))
+        round_and_deal(nc.vector.tensor_copy, w1_bf, w1_raw, slice(W1_ON_SCALAR, P))
+        xq_scales = keep.tile([P, S], U8, name="xq_scales", align_bytes=64)
+        nc.vector.tensor_copy(xq_scales[:], scale_table[:].indirect(offs_t[:]))
+        quantize_weight(w1_bf, w1_codes, w1_scales)
+        picked_words = keep.tile([P, 2 * S], U32, name="picked_words", tag="w1_bf", align_bytes=64)
+        xq_words = picked_words[:, :S]
+        hz_words = picked_words[:, S:]
+        for cols in HALVES:
+            nc.vector.tensor_copy(xq_words[:, cols], word_table[:].bitcast(U32).indirect(entries(offs_t, cols)))
+
+        y_parts = [(t, cols) for t in (0, 1) for cols in HALVES] + [(t, WHOLE) for t in (2, 3)]
+        y_banks = []
+        for t, cols in y_parts:
+            bank = psum_bank("y_bank", t, cols)
+            product(bank, w1_codes, w1_scales, t, xq_words[:, cols], xq_scales[:, cols], True, True)
+            y_banks.append(bank)
+
+        nc.vector.tensor_copy(hz_words, word_table[:].bitcast(U32).indirect(hz_t[:]))
+        hz_picked = keep.tile([P, S], U8, name="hz_picked", tag="word_table", align_bytes=64)
+        nc.vector.tensor_copy(hz_picked[:], scale_table[:].indirect(hz_t[:]))
+        for r in range(PACK):
+            source = r if r < PACK // 2 else GROUP + r
+            nc.sync.dma_start(
+                hz_scales[:].bitcast(I32)[r:P:QUADRANT, :], hz_picked[:].bitcast(I32)[source:P:QUADRANT, :]
+            )
         w2_bf, w2_codes, w2_scales = weight_tiles("w2")
         w3_bf, w3_codes, w3_scales = weight_tiles("w3")
-        deal(nc.vector.tensor_copy, w3_bf, w3_raw, slice(0, P))
+        round_and_deal(nc.vector.tensor_copy, w3_bf, w3_raw, slice(0, P))
         quantize_weight(w3_bf, w3_codes, w3_scales)
-        deal(nc.vector.tensor_copy, w2_bf, w2_raw, slice(0, P))
+        round_and_deal(nc.vector.tensor_copy, w2_bf, w2_raw, slice(0, P))
 
         window = [keep.tile([P, 2 * S], F32, name="window%d" % t) for t in range(PACK)]
-        z_rows = keep.tile([P, 2, PACK, HALF], BF16, name="z_rows", align_bytes=64)
-        units = [(0, whole), (1, whole)] + [(t, cols) for cols in halves for t in (2, 3)]
+        z_rows = keep.tile([P, len(HALVES), PACK, HALF], BF16, name="z_rows", align_bytes=64)
+
+        def empty_y_banks(plane):
+            for (t, cols), bank in zip(y_parts, y_banks):
+                if t == plane:
+                    scaled = window[t][:, S + cols.start : S + cols.stop]
+                    if (t, cols) == (1, HALVES[1]):
+                        nc.vector.tensor_copy(window[t][:, cols], bank[:])
+                        nc.vector.tensor_scalar(scaled, window[t][:, cols], gain[:, t : t + 1], None, ALU.mult)
+                    else:
+                        nc.scalar.copy(window[t][:, cols], bank[:])
+                        nc.scalar.activation(scaled, bank[:], COPY, scale=gain[:, t : t + 1])
+
+        def look_up(name, t, list_tile, cols):
+            picked = ring.tile([P, cols.stop - cols.start], F32, name=name)
+            nc.scalar.activation(picked[:], window[t][:].indirect(entries(list_tile, cols)), COPY)
+            return picked
 
         def by_half(ap):
             return ap.rearrange("p (s c) -> p s c", c=HALF)
 
-        def look_up(name, t, offsets, cols):
-            picked = ring.tile([P, cols.stop - cols.start], F32, name=name)
-            nc.scalar.activation(picked[:], window[t][:].indirect(entries(offsets, cols)), COPY)
-            return picked
-
-        def combine(u, t, cols, y2, y3, between):
-            width = cols.stop - cols.start
-            larger = keep.tile([P, width], F32, name="larger", tag=("w2_raw", "w2_bf")[u % 2], align_bytes=64)
-            nc.vector.tensor_tensor(larger[:], y2[:], y3[:], ALU.max)
-            between[0]()
-            rest = ring.tile([P, width], F32, name="rest")
-            nc.vector.tensor_tensor(rest[:], window[t][:].indirect(entries(n1_t, cols)), larger[:], ALU.subtract)
-            between[1]()
-
-            def scale():
-                nc.vector.scalar_tensor_tensor(
-                    z_rows[:, cols.start // HALF : cols.stop // HALF, t, :],
-                    by_half(rest[:]),
-                    gain[:, t : t + 1],
-                    by_half(window[t][:, S + cols.start : S + cols.stop]),
-                    ALU.mult,
-                    ALU.add,
-                )
-
-            return scale
-
-        z_codes = [keep.tile([P, HALF], U32, name="z_codes%d" % s, align_bytes=64) for s in range(2)]
-        z_scales = [keep.tile([P, HALF], U8, name="z_scales%d" % s, align_bytes=64) for s in range(2)]
-        z_bf = [keep.tile([P, HALF, PACK], BF16, name="z_bf%d" % s, align_bytes=64) for s in range(2)]
+        def finish_z(t, cols, rest):
+            nc.vector.scalar_tensor_tensor(
+                z_rows[:, cols.start // HALF : cols.stop // HALF, t, :],
+                by_half(rest[:]),
+                gain[:, t : t + 1],
+                by_half(window[t][:, S + cols.start : S + cols.stop]),
+                ALU.mult,
+                ALU.add,
+            )
 
         def interleave(copy, s):
+            z_bf = keep.tile([P, HALF, PACK], BF16, name="z_bf%d" % s, align_bytes=64)
             copy(
-                z_bf[s][:].rearrange("p (c i) t -> p c t i", i=8),
-                z_rows[:, s, :, :].rearrange("p t (c i) -> p c t i", i=8),
+                z_bf[:].rearrange("p (c i) t -> p c t i", i=LINE_BF16),
+                z_rows[:, s, :, :].rearrange("p t (c i) -> p c t i", i=LINE_BF16),
             )
+            return z_bf
 
-        def second_product(s, copies):
-            cols = halves[s]
-            nc.vector.quantize_mx(
-                out=z_codes[s][:].bitcast(FP8X4), scales=z_scales[s][:], in_=z_bf[s][:].rearrange("p c t -> p (c t)")
-            )
-            banks = []
+        def make_h(s, z_bf, copy):
+            cols = HALVES[s]
+            z_codes = keep.tile([P, HALF], U32, name="z_codes%d" % s, align_bytes=64)
+            z_scales = keep.tile([P, HALF], U8, name="z_scales%d" % s, align_bytes=64)
+            quantize(z_bf[:].rearrange("p c t -> p (c t)"), z_codes, z_scales)
             for t in range(PACK):
-                bank = psum.tile([P, HALF], F32, name="h_bank%d_%d" % (s, t), tag=("early%d", "late%d")[s] % t)
-                product(bank[:], w3_codes, w3_scales, t, hz_words[:, cols], hz_scales[:, cols], True, False)
-                product(bank[:], w2_codes, w2_scales, t, z_codes[s][:], z_scales[s][:], False, True)
-                banks.append(bank)
-                if t < len(copies):
-                    copies[t](window[t][:, cols], bank[:])
-            return banks
+                bank = psum_bank("h_bank", t, cols)
+                product(bank, w3_codes, w3_scales, t, hz_words[:, cols], hz_scales[:, cols], True, False)
+                product(bank, w2_codes, w2_scales, t, z_codes[:], z_scales[:], False, True)
+                copy(window[t][:, cols], bank[:])
 
-        def leave_bank(t):
-            for part in [c for p, c in y_parts if p == t]:
-                bank = y_bank[t, part.start]
-                if t in (1,):
-                    nc.vector.tensor_copy(window[t][:, part], bank[:])
-                else:
-                    nc.scalar.copy(window[t][:, part], bank[:])
-                if t in (1,):
-                    nc.vector.tensor_scalar(window[t][:, S:], window[t][:, :S], gain[:, t : t + 1], None, ALU.mult)
-                else:
-                    nc.scalar.activation(
-                        window[t][:, S + part.start : S + part.stop], bank[:], COPY, scale=gain[:, t : t + 1]
-                    )
-
-        def nothing():
-            return None
-
-        pending = lambda: quantize_weight(w2_bf, w2_codes, w2_scales)
-        for u, (t, cols) in enumerate(units):
-            if cols.start == 0 and t not in (1,):
-                leave_bank(t)
-            if t == 0:
-                for later in (1,):
-                    leave_bank(later)
+        z_steps = [(t, WHOLE) for t in (0, 1)] + [(t, cols) for cols in HALVES for t in (2, 3)]
+        unfinished = None
+        for step, (t, cols) in enumerate(z_steps):
+            width = cols.stop - cols.start
+            if cols.start == 0:
+                empty_y_banks(t)
             y2 = look_up("y2", t, n2_t, cols)
             y3 = look_up("y3", t, n3_t, cols)
-            pending = combine(u, t, cols, y2, y3, (pending, nothing))
-        interleave(nc.scalar.copy, 0)
-        second_product(0, [nc.scalar.copy] * PACK)
-        pending()
-        interleave(nc.vector.tensor_copy, 1)
-        late_banks = second_product(1, [nc.vector.tensor_copy] * 4)
+            larger = keep.tile([P, width], F32, name="larger", tag=("w2_raw", "w2_bf")[step % 2], align_bytes=64)
+            nc.vector.tensor_tensor(larger[:], y2[:], y3[:], ALU.max)
+            if unfinished is None:
+                quantize_weight(w2_bf, w2_codes, w2_scales)
+            else:
+                finish_z(*unfinished)
+            rest = ring.tile([P, width], F32, name="rest")
+            nc.vector.tensor_tensor(rest[:], window[t][:].indirect(entries(n1_t, cols)), larger[:], ALU.subtract)
+            unfinished = (t, cols, rest)
+        make_h(0, interleave(nc.scalar.copy, 0), nc.scalar.copy)
+        finish_z(*unfinished)
+        make_h(1, interleave(nc.vector.tensor_copy, 1), nc.vector.tensor_copy)
 
         out_rows = out.rearrange("(p t) j -> p t j", t=PACK)
-        pending = nothing
-        units = [(t, cols) for t in range(PACK) for cols in halves]
-        for t, cols in units:
-            width = cols.stop - cols.start
-            if t + 0 >= 4 and t + 0 < PACK and cols.start == 0:
-                nc.scalar.copy(window[t + 0][:, halves[1]], late_banks[t + 0][:])
-            h5 = look_up("h5", t, n5_t, cols)
-            h4 = look_up("h4", t, n4_t, cols)
-            far = ring.tile([P, width], F32, name="far")
-            nc.vector.tensor_tensor(far[:], window[t][:].indirect(entries(n6_t, cols)), h5[:], ALU.mult)
-            pending()
-            near = ring.tile([P, width], F32, name="near")
-            nc.vector.scalar_tensor_tensor(near[:], h4[:], 0.75, window[t][:, cols], ALU.mult, ALU.mult)
 
-            def store(t=t, cols=cols, width=width, far=far, near=near):
-                result = keep.tile([P, width], F32, name="result%d_%d" % (t, cols.start))
-                nc.vector.scalar_tensor_tensor(result[:], far[:], 0.75, near[:], ALU.mult, ALU.add)
-                nc.sync.dma_start(out_rows[:, t, cols], result[:])
+        def add_and_store(t, cols, far, near):
+            result = keep.tile([P, HALF], F32, name="result%d_%d" % (t, cols.start))
+            nc.vector.scalar_tensor_tensor(result[:], far[:], 0.75, near[:], ALU.mult, ALU.add)
+            nc.sync.dma_start(out_rows[:, t, cols], result[:])
 
-            pending = store
-        pending()
+        unstored = None
+        for t in range(PACK):
+            for cols in HALVES:
+                h5 = look_up("h5", t, n5_t, cols)
+                h4 = look_up("h4", t, n4_t, cols)
+                far = ring.tile([P, HALF], F32, name="far")
+                nc.vector.tensor_tensor(far[:], window[t][:].indirect(entries(n6_t, cols)), h5[:], ALU.mult)
+                if unstored is not None:
+                    add_and_store(*unstored)
+                near = ring.tile([P, HALF], F32, name="near")
+                nc.vector.scalar_tensor_tensor(near[:], h4[:], 0.75, window[t][:, cols], ALU.mult, ALU.mult)
+                unstored = (t, cols, far, near)
+        add_and_store(*unstored)

@@ -24,7 +24,7 @@ WHOLE = slice(0, S)
 HALVES = (slice(0, HALF), slice(HALF, S))
 LINE_BF16 = 8
 RING = 3
-W1_ON_SCALAR = 96
+W1_ON_SCALAR = 56
 
 
 def tile_picked_mixhtrimdot_none_p_kernel(
@@ -56,7 +56,7 @@ def tile_picked_mixhtrimdot_none_p_kernel(
         nc.gpsimd.memset(hz_scales[:].bitcast(I32), 0)
 
         offs_t = load_list("offs_t", offs)
-        w1_raw = load_weight("w1_raw", w1)
+        hz_t = load_list("hz_t", hz)
         scale_rows = x_scales[0].bitcast(I32)
         table_rows = scale_table[:].bitcast(I32)
         for r in range(PACK // 2):
@@ -64,9 +64,9 @@ def tile_picked_mixhtrimdot_none_p_kernel(
         for r in range(PACK // 2, PACK):
             twice = scale_rows[r:16:PACK, :].unsqueeze(1).broadcast_to([P // QUADRANT, 2, T // 4])
             nc.sync.dma_start(table_rows[r:P:GROUP, :], twice)
+        w1_raw = load_weight("w1_raw", w1)
         word_table = keep.tile([P, T], I32, name="word_table", align_bytes=64)
         nc.sync.dma_start(word_table[:], x_words[0].rearrange("p n t -> p (n t)").bitcast(I32))
-        hz_t = load_list("hz_t", hz)
         gain = keep.tile([P, PACK], F32, name="gain")
         nc.sync.dma_start(gain[:], gn.rearrange("(p t) o -> p (t o)", t=PACK))
         n2_t = load_list("n2_t", n2)
@@ -113,11 +113,18 @@ def tile_picked_mixhtrimdot_none_p_kernel(
             tag = ("first%d" if cols.stop < S else "second%d") % t
             return psum.tile([P, cols.stop - cols.start], F32, name=name, tag=tag)
 
+        xq_scales = keep.tile([P, S], U8, name="xq_scales", align_bytes=64)
+        nc.vector.tensor_copy(xq_scales[:], scale_table[:].indirect(offs_t[:]))
+        hz_picked = keep.tile([P, S], U8, name="hz_picked", align_bytes=64)
+        nc.vector.tensor_copy(hz_picked[:], scale_table[:].indirect(hz_t[:]))
+        for r in range(PACK):
+            source = r if r < PACK // 2 else GROUP + r
+            nc.sync.dma_start(
+                hz_scales[:].bitcast(I32)[r:P:QUADRANT, :], hz_picked[:].bitcast(I32)[source:P:QUADRANT, :]
+            )
         w1_bf, w1_codes, w1_scales = weight_tiles("w1")
         round_and_deal(nc.scalar.copy, w1_bf, w1_raw, slice(0, W1_ON_SCALAR))
         round_and_deal(nc.vector.tensor_copy, w1_bf, w1_raw, slice(W1_ON_SCALAR, P))
-        xq_scales = keep.tile([P, S], U8, name="xq_scales", align_bytes=64)
-        nc.vector.tensor_copy(xq_scales[:], scale_table[:].indirect(offs_t[:]))
         quantize_weight(w1_bf, w1_codes, w1_scales)
         picked_words = keep.tile([P, 2 * S], U32, name="picked_words", tag="w1_bf", align_bytes=64)
         xq_words = picked_words[:, :S]
@@ -125,7 +132,7 @@ def tile_picked_mixhtrimdot_none_p_kernel(
         for cols in HALVES:
             nc.vector.tensor_copy(xq_words[:, cols], word_table[:].bitcast(U32).indirect(entries(offs_t, cols)))
 
-        y_parts = [(t, cols) for t in (0, 1) for cols in HALVES] + [(t, WHOLE) for t in (2, 3)]
+        y_parts = [(0, cols) for cols in HALVES] + [(t, WHOLE) for t in (1, 2, 3)]
         y_banks = []
         for t, cols in y_parts:
             bank = psum_bank("y_bank", t, cols)
@@ -133,18 +140,11 @@ def tile_picked_mixhtrimdot_none_p_kernel(
             y_banks.append(bank)
 
         nc.vector.tensor_copy(hz_words, word_table[:].bitcast(U32).indirect(hz_t[:]))
-        hz_picked = keep.tile([P, S], U8, name="hz_picked", tag="word_table", align_bytes=64)
-        nc.vector.tensor_copy(hz_picked[:], scale_table[:].indirect(hz_t[:]))
-        for r in range(PACK):
-            source = r if r < PACK // 2 else GROUP + r
-            nc.sync.dma_start(
-                hz_scales[:].bitcast(I32)[r:P:QUADRANT, :], hz_picked[:].bitcast(I32)[source:P:QUADRANT, :]
-            )
         w2_bf, w2_codes, w2_scales = weight_tiles("w2")
         w3_bf, w3_codes, w3_scales = weight_tiles("w3")
         round_and_deal(nc.vector.tensor_copy, w3_bf, w3_raw, slice(0, P))
-        quantize_weight(w3_bf, w3_codes, w3_scales)
         round_and_deal(nc.vector.tensor_copy, w2_bf, w2_raw, slice(0, P))
+        quantize_weight(w3_bf, w3_codes, w3_scales)
 
         window = [keep.tile([P, 2 * S], F32, name="window%d" % t) for t in range(PACK)]
         z_rows = keep.tile([P, len(HALVES), PACK, HALF], BF16, name="z_rows", align_bytes=64)
@@ -153,7 +153,7 @@ def tile_picked_mixhtrimdot_none_p_kernel(
             for (t, cols), bank in zip(y_parts, y_banks):
                 if t == plane:
                     scaled = window[t][:, S + cols.start : S + cols.stop]
-                    if (t, cols) == (1, HALVES[1]):
+                    if t == 1:
                         nc.vector.tensor_copy(window[t][:, cols], bank[:])
                         nc.vector.tensor_scalar(scaled, window[t][:, cols], gain[:, t : t + 1], None, ALU.mult)
                     else:

@@ -186,16 +186,20 @@ def tile_picked_mixhtrimdot_none_p_kernel(
             )
             return z_bf
 
-        def make_h(s, z_bf, copy):
+        def make_h(s, z_bf, copy, planes):
             cols = HALVES[s]
             z_codes = keep.tile([P, HALF], U32, name="z_codes%d" % s, align_bytes=64)
             z_scales = keep.tile([P, HALF], U8, name="z_scales%d" % s, align_bytes=64)
             quantize(z_bf[:].rearrange("p c t -> p (c t)"), z_codes, z_scales)
+            banks = []
             for t in range(PACK):
                 bank = psum_bank("h_bank", t, cols)
                 product(bank, w3_codes, w3_scales, t, hz_words[:, cols], hz_scales[:, cols], True, False)
                 product(bank, w2_codes, w2_scales, t, z_codes[:], z_scales[:], False, True)
-                copy(window[t][:, cols], bank[:])
+                banks.append(bank)
+                if t < planes:
+                    copy(window[t][:, cols], bank[:])
+            return banks
 
         z_steps = [(t, WHOLE) for t in (0, 1)] + [(t, cols) for cols in HALVES for t in (2, 3)]
         unfinished = None
@@ -214,9 +218,9 @@ def tile_picked_mixhtrimdot_none_p_kernel(
             rest = ring.tile([P, width], F32, name="rest")
             nc.vector.tensor_tensor(rest[:], window[t][:].indirect(entries(n1_t, cols)), larger[:], ALU.subtract)
             unfinished = (t, cols, rest)
-        make_h(0, interleave(nc.scalar.copy, 0), nc.scalar.copy)
+        make_h(0, interleave(nc.scalar.copy, 0), nc.scalar.copy, PACK)
         finish_z(*unfinished)
-        make_h(1, interleave(nc.vector.tensor_copy, 1), nc.vector.tensor_copy)
+        late_banks = make_h(1, interleave(nc.vector.tensor_copy, 1), nc.vector.tensor_copy, 2)
 
         out_rows = out.rearrange("(p t) j -> p t j", t=PACK)
 
@@ -228,13 +232,22 @@ def tile_picked_mixhtrimdot_none_p_kernel(
         unstored = None
         for t in range(PACK):
             for cols in HALVES:
+                if t in (1, 2) and cols == HALVES[1]:
+                    nc.scalar.copy(window[t + 1][:, cols], late_banks[t + 1][:])
                 h5 = look_up("h5", t, n5_t, cols)
-                h4 = look_up("h4", t, n4_t, cols)
+                if unstored is None:
+                    h4 = ring.tile([P, HALF], F32, name="h4")
+                    nc.vector.tensor_copy(h4[:], window[t][:].indirect(entries(n4_t, cols)))
+                else:
+                    h4 = look_up("h4", t, n4_t, cols)
                 far = ring.tile([P, HALF], F32, name="far")
                 nc.vector.tensor_tensor(far[:], window[t][:].indirect(entries(n6_t, cols)), h5[:], ALU.mult)
-                if unstored is not None:
+                last = (t, cols) == (PACK - 1, HALVES[1])
+                if unstored is not None and not last:
                     add_and_store(*unstored)
                 near = ring.tile([P, HALF], F32, name="near")
                 nc.vector.scalar_tensor_tensor(near[:], h4[:], 0.75, window[t][:, cols], ALU.mult, ALU.mult)
+                if last:
+                    add_and_store(*unstored)
                 unstored = (t, cols, far, near)
         add_and_store(*unstored)

from contextlib import ExitStack

import concourse.mybir as mybir

K, T, S, H, N = 512, 2048, 512, 512, 512
FLOPS = 2 * S * (K * H + H * N + K * N)

F32 = mybir.dt.float32
BF16 = mybir.dt.bfloat16
I32 = mybir.dt.int32
U32 = mybir.dt.uint32
U16 = mybir.dt.uint16
U8 = mybir.dt.uint8
FP8X4 = mybir.dt.float8_e4m3fn_x4
ALU = mybir.AluOpType
COPY = mybir.ActivationFunctionType.Copy

P = 128
PACK = 4
QUADRANT = 32
GROUP = 16
HALF = S // 2
WHOLE = slice(0, S)
HALVES = (slice(0, HALF), slice(HALF, S))
LINE_BF16 = 8
RING = 3
W1_ON_SCALAR = 56


def tile_picked_mixhtrimdot_none_p_kernel(
    tc, x_words, x_scales, w1, gn, w2, w3, offs, n1, n2, n3, hz, n4, n5, n6, out
):
    nc = tc.nc
    with ExitStack() as ctx:
        lists = ctx.enter_context(tc.tile_pool(name="lists", bufs=1))
        keep = ctx.enter_context(tc.tile_pool(name="keep", bufs=1))
        ring = ctx.enter_context(tc.tile_pool(name="ring", bufs=RING))
        psum = ctx.enter_context(tc.psum_pool(name="psum", bufs=1))

        def load_list(name, dram):
            tile = lists.tile([P, S // GROUP], U16, name=name)
            nc.sync.dma_start(tile[:], dram)
            return tile

        def load_weight(name, dram):
            raw = keep.tile([P, PACK, dram.shape[1]], F32, name=name, align_bytes=64)
            nc.sync.dma_start(raw[:], dram.rearrange("(p j) c -> p j c", j=PACK))
            return raw

        def entries(list_tile, cols):
            return list_tile[:, cols.start // GROUP : cols.stop // GROUP]

        scale_table = keep.tile([P, T], U8, name="scale_table", align_bytes=64)
        nc.gpsimd.memset(scale_table[:].bitcast(I32), 0)
        hz_scales = keep.tile([P, S], U8, name="hz_scales", align_bytes=64)
        nc.gpsimd.memset(hz_scales[:].bitcast(I32), 0)

        offs_t = load_list("offs_t", offs)
        hz_t = load_list("hz_t", hz)
        scale_rows = x_scales[0].bitcast(I32)
        table_rows = scale_table[:].bitcast(I32)
        for r in range(PACK // 2):
            nc.sync.dma_start(table_rows[r:P:QUADRANT, :], scale_rows[r:16:PACK, :])
        for r in range(PACK // 2, PACK):
            twice = scale_rows[r:16:PACK, :].unsqueeze(1).broadcast_to([P // QUADRANT, 2, T // 4])
            nc.sync.dma_start(table_rows[r:P:GROUP, :], twice)
        w1_raw = load_weight("w1_raw", w1)
        word_table = keep.tile([P, T], I32, name="word_table", align_bytes=64)
        nc.sync.dma_start(word_table[:], x_words[0].rearrange("p n t -> p (n t)").bitcast(I32))
        gain = keep.tile([P, PACK], F32, name="gain")
        nc.sync.dma_start(gain[:], gn.rearrange("(p t) o -> p (t o)", t=PACK))
        n2_t = load_list("n2_t", n2)
        n3_t = load_list("n3_t", n3)
        n1_t = load_list("n1_t", n1)
        w3_raw = load_weight("w3_raw", w3)
        w2_raw = load_weight("w2_raw", w2)
        n4_t = load_list("n4_t", n4)
        n5_t = load_list("n5_t", n5)
        n6_t = load_list("n6_t", n6)

        def weight_tiles(name):
            return (
                keep.tile([P, PACK, P, PACK], BF16, name=name + "_bf", align_bytes=64),
                keep.tile([P, PACK * P], U32, name=name + "_codes", align_bytes=64),
                keep.tile([P, PACK * P], U8, name=name + "_scales", align_bytes=64),
            )

        def round_and_deal(copy, rounded, raw, m):
            copy(
                rounded[:, :, m, :].rearrange("p t m j -> p m j t"),
                raw[:].rearrange("p j (m t) -> p m j t", t=PACK)[:, m, :, :],
            )

        def quantize(rounded, codes, scales):
            nc.vector.quantize_mx(out=codes[:].bitcast(FP8X4), scales=scales[:], in_=rounded)

        def quantize_weight(rounded, codes, scales):
            quantize(rounded[:].rearrange("p t m j -> p (t m j)"), codes, scales)

        def product(bank, codes, scales, t, words, word_scales, start, stop):
            m = slice(t * P, (t + 1) * P)
            nc.tensor.matmul_mx(
                out=bank[:],
                lhsT=codes[:, m].bitcast(FP8X4),
                lhsT_scale=scales[:, m],
                rhs=words.bitcast(FP8X4),
                rhs_scale=word_scales,
                start=start,
                stop=stop,
            )

        def psum_bank(name, t, cols):
            tag = ("first%d" if cols.stop < S else "second%d") % t
            return psum.tile([P, cols.stop - cols.start], F32, name=name, tag=tag)

        xq_scales = keep.tile([P, S], U8, name="xq_scales", align_bytes=64)
        nc.vector.tensor_copy(xq_scales[:], scale_table[:].indirect(offs_t[:]))
        hz_picked = keep.tile([P, S], U8, name="hz_picked", align_bytes=64)
        nc.vector.tensor_copy(hz_picked[:], scale_table[:].indirect(hz_t[:]))
        for r in range(PACK):
            source = r if r < PACK // 2 else GROUP + r
            nc.sync.dma_start(
                hz_scales[:].bitcast(I32)[r:P:QUADRANT, :], hz_picked[:].bitcast(I32)[source:P:QUADRANT, :]
            )
        w1_bf, w1_codes, w1_scales = weight_tiles("w1")
        round_and_deal(nc.scalar.copy, w1_bf, w1_raw, slice(0, W1_ON_SCALAR))
        round_and_deal(nc.vector.tensor_copy, w1_bf, w1_raw, slice(W1_ON_SCALAR, P))
        quantize_weight(w1_bf, w1_codes, w1_scales)
        picked_words = keep.tile([P, 2 * S], U32, name="picked_words", tag="w1_bf", align_bytes=64)
        xq_words = picked_words[:, :S]
        hz_words = picked_words[:, S:]
        for cols in HALVES:
            nc.vector.tensor_copy(xq_words[:, cols], word_table[:].bitcast(U32).indirect(entries(offs_t, cols)))

        y_parts = [(0, cols) for cols in HALVES] + [(t, WHOLE) for t in (1, 2, 3)]
        y_banks = []
        for t, cols in y_parts:
            bank = psum_bank("y_bank", t, cols)
            product(bank, w1_codes, w1_scales, t, xq_words[:, cols], xq_scales[:, cols], True, True)
            y_banks.append(bank)

        nc.vector.tensor_copy(hz_words, word_table[:].bitcast(U32).indirect(hz_t[:]))
        w2_bf, w2_codes, w2_scales = weight_tiles("w2")
        w3_bf, w3_codes, w3_scales = weight_tiles("w3")
        round_and_deal(nc.vector.tensor_copy, w3_bf, w3_raw, slice(0, P))
        round_and_deal(nc.vector.tensor_copy, w2_bf, w2_raw, slice(0, P))
        quantize_weight(w3_bf, w3_codes, w3_scales)

        window = [keep.tile([P, 2 * S], F32, name="window%d" % t) for t in range(PACK)]
        z_rows = keep.tile([P, len(HALVES), PACK, HALF], BF16, name="z_rows", align_bytes=64)

        def empty_y_banks(plane):
            for (t, cols), bank in zip(y_parts, y_banks):
                if t == plane:
                    scaled = window[t][:, S + cols.start : S + cols.stop]
                    if t == 1:
                        nc.vector.tensor_copy(window[t][:, cols], bank[:])
                        nc.vector.tensor_scalar(scaled, window[t][:, cols], gain[:, t : t + 1], None, ALU.mult)
                    else:
                        nc.scalar.copy(window[t][:, cols], bank[:])
                        nc.scalar.activation(scaled, bank[:], COPY, scale=gain[:, t : t + 1])

        def look_up(name, t, list_tile, cols):
            picked = ring.tile([P, cols.stop - cols.start], F32, name=name)
            nc.scalar.activation(picked[:], window[t][:].indirect(entries(list_tile, cols)), COPY)
            return picked

        def by_half(ap):
            return ap.rearrange("p (s c) -> p s c", c=HALF)

        def finish_z(t, cols, rest):
            nc.vector.scalar_tensor_tensor(
                z_rows[:, cols.start // HALF : cols.stop // HALF, t, :],
                by_half(rest[:]),
                gain[:, t : t + 1],
                by_half(window[t][:, S + cols.start : S + cols.stop]),
                ALU.mult,
                ALU.add,
            )

        def interleave(copy, s):
            z_bf = keep.tile([P, HALF, PACK], BF16, name="z_bf%d" % s, align_bytes=64)
            copy(
                z_bf[:].rearrange("p (c i) t -> p c t i", i=LINE_BF16),
                z_rows[:, s, :, :].rearrange("p t (c i) -> p c t i", i=LINE_BF16),
            )
            return z_bf

        def make_h(s, z_bf, copy, planes):
            cols = HALVES[s]
            z_codes = keep.tile([P, HALF], U32, name="z_codes%d" % s, align_bytes=64)
            z_scales = keep.tile([P, HALF], U8, name="z_scales%d" % s, align_bytes=64)
            quantize(z_bf[:].rearrange("p c t -> p (c t)"), z_codes, z_scales)
            banks = []
            for t in range(PACK):
                bank = psum_bank("h_bank", t, cols)
                product(bank, w3_codes, w3_scales, t, hz_words[:, cols], hz_scales[:, cols], True, False)
                product(bank, w2_codes, w2_scales, t, z_codes[:], z_scales[:], False, True)
                banks.append(bank)
                if t < planes:
                    copy(window[t][:, cols], bank[:])
            return banks

        z_steps = [(t, WHOLE) for t in (0, 1)] + [(t, cols) for cols in HALVES for t in (2, 3)]
        unfinished = None
        for step, (t, cols) in enumerate(z_steps):
            width = cols.stop - cols.start
            if cols.start == 0:
                empty_y_banks(t)
            y2 = look_up("y2", t, n2_t, cols)
            y3 = look_up("y3", t, n3_t, cols)
            larger = keep.tile([P, width], F32, name="larger", tag=("w2_raw", "w2_bf")[step % 2], align_bytes=64)
            nc.vector.tensor_tensor(larger[:], y2[:], y3[:], ALU.max)
            if unfinished is None:
                quantize_weight(w2_bf, w2_codes, w2_scales)
            else:
                finish_z(*unfinished)
            rest = ring.tile([P, width], F32, name="rest")
            nc.vector.tensor_tensor(rest[:], window[t][:].indirect(entries(n1_t, cols)), larger[:], ALU.subtract)
            unfinished = (t, cols, rest)
        make_h(0, interleave(nc.scalar.copy, 0), nc.scalar.copy, PACK)
        finish_z(*unfinished)
        late_banks = make_h(1, interleave(nc.vector.tensor_copy, 1), nc.vector.tensor_copy, 2)

        out_rows = out.rearrange("(p t) j -> p t j", t=PACK)

        def add_and_store(t, cols, far, near):
            result = keep.tile([P, HALF], F32, name="result%d_%d" % (t, cols.start))
            nc.vector.scalar_tensor_tensor(result[:], far[:], 0.75, near[:], ALU.mult, ALU.add)
            nc.sync.dma_start(out_rows[:, t, cols], result[:])

        unstored = None
        for t in range(PACK):
            for cols in HALVES:
                if t in (1, 2) and cols == HALVES[1]:
                    nc.scalar.copy(window[t + 1][:, cols], late_banks[t + 1][:])
                h5 = look_up("h5", t, n5_t, cols)
                if unstored is None:
                    h4 = ring.tile([P, HALF], F32, name="h4")
                    nc.vector.tensor_copy(h4[:], window[t][:].indirect(entries(n4_t, cols)))
                else:
                    h4 = look_up("h4", t, n4_t, cols)
                far = ring.tile([P, HALF], F32, name="far")
                nc.vector.tensor_tensor(far[:], window[t][:].indirect(entries(n6_t, cols)), h5[:], ALU.mult)
                last = (t, cols) == (PACK - 1, HALVES[1])
                if unstored is not None and not last:
                    add_and_store(*unstored)
                near = ring.tile([P, HALF], F32, name="near")
                nc.vector.scalar_tensor_tensor(near[:], h4[:], 0.75, window[t][:, cols], ALU.mult, ALU.mult)
                if last:
                    add_and_store(*unstored)
                unstored = (t, cols, far, near)
        add_and_store(*unstored)
